import numpy as np, ml_dtypes
CORES = [23,119,17,113]
N = 4
import mx_ref
BF = ml_dtypes.bfloat16
def entries(a):
    return np.ascontiguousarray(a.T).reshape(-1)
def table(e):
    return np.ascontiguousarray(np.reshape(e, (-1, 16)).T).astype(np.int32)
def cols(t, e):
    v = np.concatenate([t.reshape(128, -1, 4), np.zeros((128, 1, 4), BF)], axis=1)
    return np.ascontiguousarray(v[:, e]).reshape(128, -1)
def f(rng, *shape):
    return mx_ref.flush((rng.standard_normal(shape, dtype=np.float32) * np.exp2(rng.integers(-2, 3, shape[:-1] + (1,)))).astype(BF))
def wide(rng, *shape, cols=0):
    v = rng.standard_normal(shape, dtype=np.float32) * np.exp2(rng.integers(-12, 13, shape)).astype(np.float32)
    if cols: v *= np.repeat(np.exp2(rng.integers(-cols, cols + 1, shape[:-2] + (1, shape[-1] // 4))) * (rng.random(shape[:-2] + (1, shape[-1] // 4)) > 0.0625), 4, axis=-1).astype(np.float32)
    return mx_ref.flush(v.astype(BF))
T, CAPP = 512, 192
def lists(rng, full=False, skew=False, single=False, back=False):
    if full:
        v = rng.permutation(([CAPP] * (T // CAPP) + [T % CAPP] + [0] * N)[:N])
        n = v[(np.arange(N)[None, :] - np.arange(N)[:, None]) % N][rng.permutation(N)][:, rng.permutation(N)]
    else:
        n = np.full((N, N), T // N)
        for _ in range(20 * N):
            (s, t), (d, e) = rng.permutation(N)[:2], rng.permutation(N)[:2]
            k = rng.integers(0, min(n[s, d], n[t, e], CAPP - n[s, e], CAPP - n[t, d]) + 1)
            n[s, d] -= k; n[t, e] -= k; n[s, e] += k; n[t, d] += k
    a = np.full((N, N * CAPP), -1)
    for s in range(N):
        parts = np.split(rng.permutation(T), np.cumsum(n[s])[:-1])
        for d in range(N): a[s, d * CAPP + rng.permutation(CAPP)[:n[s, d]]] = parts[d]
    p, u, o = [], [], []
    for r in range(N):
        used = np.flatnonzero(a[:, r * CAPP:(r + 1) * CAPP].reshape(-1) >= 0)
        p.append(table(used[::-1] if back else rng.permutation(used)))
        h = rng.integers(0, N)
        c = rng.integers(0, 2, N) if full else (np.full(N, -1) if rng.random() < 0.5 else rng.integers(0, 2, N)) if single else rng.integers(-1, 2, N)
        if c[h] < 0: c[h] = rng.integers(0, 2)
        named = np.flatnonzero(c >= 0)
        if single: named = np.array([h])
        if skew:
            m = rng.integers(T // 2 + 1, T + 1)
            e = np.sort(np.concatenate([np.full(m, h), rng.choice(named, T - m)]))
        elif full: e = np.sort(np.concatenate([named, rng.choice(named, T - N)]))
        else: e = np.repeat(named, np.diff(np.concatenate([[0], np.sort(rng.integers(0, T + 1, len(named) - 1)), [T]])))
        u.append(table(np.concatenate([c, np.full(16 - N, -1)]))); o.append(table(e))
    return {"send": np.stack([table(k) for k in a]), "place": np.stack(p), "sel": np.stack(u), "of": np.stack(o)}
def setup_inputs(rng):
    return {"x": f(rng, N, 128, 4 * T), "w": f(rng, N, 256, 512), **lists(rng)}
def setup_inputs_full(rng):
    return {**setup_inputs(rng), **lists(rng, full=True)}
def setup_inputs_reversed(rng):
    return {**setup_inputs(rng), **lists(rng, back=True)}
def setup_inputs_single(rng):
    return {**setup_inputs(rng), **lists(rng, single=True)}
def setup_inputs_skew(rng):
    return {**setup_inputs(rng), **lists(rng, skew=True)}
def setup_inputs_spread(rng):
    d = setup_inputs(rng); d["x"] = wide(rng, N, 128, 4 * T, cols=8); return d
def check_inputs(d):
    b = []
    for k in ("x", "w"):
        a = np.abs(d[k].astype(np.float32))
        if not ((a == 0) | ((a >= 2.0 ** -30) & (a <= 2.0 ** 30))).all(): b.append(k)
    sends = np.stack([entries(d["send"][r]) for r in range(N)])
    for r in range(N):
        c, p, u, e = sends[r], entries(d["place"][r]), entries(d["sel"][r]), entries(d["of"][r])
        if c.min() < -1 or not np.array_equal(np.sort(c[c >= 0]), np.arange(T)): b.append("send")
        if not np.array_equal(np.sort(p), np.flatnonzero(sends[:, r * CAPP:(r + 1) * CAPP].reshape(-1) >= 0)): b.append("place")
        if u.min() < -1 or u.max() > 1 or (u[N:] != -1).any(): b.append("sel")
        if e.min() < 0 or e.max() >= N or (np.diff(e) < 0).any() or (u[e] < 0).any(): b.append("of")
    return b
def reference(x, w, send, place, sel, of):
    W = [[mx_ref.quantize(w[h][128 * m:128 * m + 128]) for m in range(2)] for h in range(N)]
    y = np.zeros((N, 128, T), np.float32)
    for r in range(N):
        slots = np.concatenate([cols(x[s], entries(send[s])[r * CAPP:(r + 1) * CAPP]) for s in range(N)], axis=1)
        X = mx_ref.quantize(cols(slots, entries(place[r])))
        u, e = entries(sel[r]), entries(of[r])
        for h in range(N):
            i = e == h
            if i.any(): y[r][:, i] = mx_ref.matmul(W[h][u[h]], X)[:, i]
    return {"y": y}

@@ -1,0 +1,274 @@
+from concourse.bass import DstId, RemoteDMATransfer
+from concourse.mybir import dt, AluOpType, ActivationFunctionType
+
+CAP = 192
+NX = 512
+EX = 128
+SL = 4 * CAP
+EV, OV = 4 * EX, 4 * CAP
+
+E_A, E_B, E_P = 0, 2 * EX, 3 * EX
+SECOND = 4
+
+CODE = "float8_e4m3fn_x4"
+SCRATCH = {
+    "raws": ("sbuf", [32, 48], "int32"),
+    "rawp": ("sbuf", [32, 32], "int32"),
+    "rawo": ("sbuf", [32, 32], "int32"),
+    "selr": ("sbuf", [128, 16], "int32"),
+    "self1": ("sbuf", [128, 16], "float32"),
+    "selm": ("sbuf", [128, 16], "float32"),
+    "sela": ("sbuf", [128, 1], "float32"),
+    "ia": ("sbuf", [128, 32], "int32"),
+    "ib": ("sbuf", [128, 32], "int32"),
+    "ic": ("sbuf", [128, 32], "int32"),
+    "base": ("sbuf", [128, 32], "float32"),
+    "off": ("sbuf", [128, 48], "uint16"),
+    "offo": ("sbuf", [128, 32], "uint16"),
+    "offp": ("sbuf", [128, 32], "uint16"),
+    "offb": ("sbuf", [128, 32], "uint16"),
+    "offy": ("sbuf", [128, 32], "uint16"),
+    "t1": ("sbuf", [32, 32], "float32"),
+    "t2": ("sbuf", [32, 32], "float32"),
+    "t3": ("sbuf", [32, 32], "float32"),
+    "t4": ("sbuf", [32, 32], "float32"),
+    "msgp": ("sbuf", [128, 1], "float32"),
+    "msgb": ("sbuf", [128, 1], "float32"),
+    "xt": ("sbuf", [128, 4 * NX], "bfloat16"),
+    "wt": ("sbuf", [128, 2 * EV], "bfloat16"),
+    "ho": ("sbuf", [128, EV], "bfloat16"),
+    "he": ("sbuf", [128, 2 * EV], "bfloat16"),
+    "ha": ("sbuf", [128, OV], "bfloat16"),
+    "hbp": ("sbuf", [128, 2 * OV], "bfloat16"),
+    "hx": ("sbuf", [128, OV], "bfloat16"),
+    "qw": ("sbuf", [128, 2 * EX], CODE), "sw": ("sbuf", [128, 2 * EX], "uint8"),
+    "qe": ("sbuf", [128, 2 * EX], CODE), "se": ("sbuf", [128, 2 * EX], "uint8"),
+    "qo": ("sbuf", [128, EX], CODE), "so": ("sbuf", [128, EX], "uint8"),
+    "qa": ("sbuf", [128, CAP], CODE), "sa": ("sbuf", [128, CAP], "uint8"),
+    "qbp": ("sbuf", [128, 2 * CAP], CODE), "sbp": ("sbuf", [128, 2 * CAP], "uint8"),
+    "le": ("sbuf", [128, 4 * EX], CODE), "les": ("sbuf", [128, 4 * EX], "uint8"),
+    "lc": ("sbuf", [128, SL], CODE), "lcs": ("sbuf", [128, SL], "uint8"),
+    "win": ("sbuf", [128, 5 * SL], "float32"),
+    "yt": ("sbuf", [128, NX], "float32"),
+}
+for _k in range(8):
+    SCRATCH["ps%d" % _k] = ("psum", [128, 512], "float32")
+
+SEMAPHORES = ["ld_sel", "ld_send", "ld_w", "ld_x", "ld_pl", "st_a", "st_b",
+              "io", "io2", "bas", "sf", "sm", "off", "offo", "offp", "offb", "offy", "sel_a",
+              "t1d", "t2d", "t3d", "t4d",
+              "q_w", "q_e", "q_o", "q_a", "q_bp", "q_x",
+              "g_o", "g_a", "g_bp", "g_e", "g_x", "g_y1", "g_y2",
+              "sent", "a_mp", "a_mb", "a_e", "a_a", "a_p", "a_b", "a_eb", "a_ep",
+              "ev1", "ev2", "ev3", "ev4"] + ["mm%d" % k for k in range(10)]
+
+
+def rank_program(g, core, T, topo):
+    rank = T.rank_of(core)
+    if rank is None:
+        return
+    S = T.sem
+    V, A_, TE, SY = g.vector, g.scalar, g.tensor, g.sync
+    op = AluOpType
+    copy = ActivationFunctionType.Copy
+
+    others = [d for d in range(len(T.cores)) if d != rank]
+    P = [d for d in others if topo.chip(T.cores[d]) == topo.chip(core)][0]
+    far = [d for d in others if d != P]
+    A = [d for d in far if topo.die(T.cores[d]) == topo.die(core)][0]
+    B = [d for d in far if d != A][0]
+    assert abs(rank - A) == 1 and abs(B - P) == 1
+    oa, bp = min(rank, A), min(B, P)
+    jb, jp = CAP * (B - bp), CAP * (P - bp)
+    eng_far = topo.engines(core, T.cores[B])
+    eng_p = [e for e in topo.engines(core, T.cores[P]) if e not in eng_far]
+    m_far = sum(1 << e for e in eng_far)
+    m_p = sum(1 << e for e in eng_p)
+    nf, npe = len(eng_far), len(eng_p)
+
+    def dst(d):
+        rid, pid, _ = topo.addr(T.cores[d])
+        return rid, pid
+
+    def vec(inst, sem, n=1):
+        inst.then_inc(S[sem], n)
+
+    SY.dma_start(T.selr[0:1, 0:16], T.sel[:]).then_inc(S.ld_sel, 16)
+    A_.dma_start(T.raws[16:32, :], T.send[:]).then_inc(S.ld_send, 16)
+    SY.dma_start(T.raws[0:16, :], T.send[:]).then_inc(S.ld_send, 16)
+    A_.dma_start(T.rawp[0:16, :], T.place[:]).then_inc(S.ld_pl, 16)
+    SY.dma_start(T.rawp[16:32, :], T.place[:]).then_inc(S.ld_pl, 16)
+    A_.dma_start(T.rawo[0:16, :], T.of[:]).then_inc(S.ld_pl, 16)
+    for k in range(2):
+        SY.dma_start(T.wt[:, EV * k:EV * k + EV], T.w[128 * k:128 * k + 128, :]).then_inc(S.ld_w, 16)
+    A_.dma_start(T.rawo[16:32, :], T.of[:]).then_inc(S.ld_pl, 16)
+    SY.dma_start(T.xt[:], T.x[:]).then_inc(S.ld_x, 16)
+
+    g.iota(T.ia[:], [[16, 32]], 0, 1).then_inc(S["io"], 1)
+    g.iota(T.ic[:], [[16, 32]], 0, 0).then_inc(S.io2, 1)
+    V.wait_ge(S["io"], 1)
+    vec(V.tensor_scalar(T.ib[:], T.ia[:], 15, None, op.bitwise_and), "bas")
+    V.wait_ge(S["bas"], 1)
+    V.wait_ge(S.io2, 1)
+    vec(V.tensor_tensor(T.base[:], T.ib[:], T.ic[:], op.add), "bas")
+
+    V.wait_ge(S.ld_sel, 16)
+    vec(V.tensor_scalar(T.self1[0:1, :], T.selr[0:1, :], 0.0, float(EV), op.max, op.mult), "sf")
+    g.wait_ge(S.sf, 1)
+    g.partition_broadcast(T.selm[:], T.self1[0:1, :], 128).then_inc(S.sm, 1)
+    g.wait_ge(S.sm, 1)
+    for d, msg, rsem, mask in ((B, T.msgb, S.a_mb, m_far), (P, T.msgp, S.a_mp, m_p)):
+        rid, pid = dst(d)
+        g.remote_dma(msg[:], T.selm[:, d:d + 1], rsem, S.sent, pid, rid, mask)
+    n_sent = [nf + npe]
+
+    def ship(d, lq, ls, l0, q, s, n, rsem):
+        rid, pid = dst(d)
+        g.remote_dma(lq[:, l0:l0 + n].bitcast(dt.uint8), q[:, 0:n].bitcast(dt.uint8), rsem, S.sent, pid, rid, m_far)
+        g.remote_dma(ls[:, l0:l0 + n], s[:, 0:n], rsem, S.sent, pid, rid, m_far)
+        n_sent[0] += 2 * nf
+
+    def ship_bp(lq, ls, q, s, n, from_to):
+        for src, land, codes in ((q, lq, True), (s, ls, False)):
+            tr = []
+            for d, m, (j, l, rs) in zip((B, P), (m_far, m_p), from_to):
+                a, b = src[:, j:j + n], land[:, l:l + n]
+                if codes:
+                    a, b = a.bitcast(dt.uint8), b.bitcast(dt.uint8)
+                rid, pid = dst(d)
+                tr.append(RemoteDMATransfer(dst_ids=[DstId(rid=rid, pnc=pid)], dma_engine_mask=m, remote_sem=rs,
+                                            src=a, dst=b))
+            g.remote_dma_fused(tr, local_sem=S.sent)
+        n_sent[0] += 2 * (nf + npe)
+
+    V.wait_ge(S.ld_send, 32)
+    for a in range(4):
+        vec(V.tensor_scalar(T.off[32 * a:32 * a + 32, :], T.raws[:], 4.0, 0.0, op.mult, op.max), "off")
+    V.wait_ge(S.ld_w, 32)
+    vec(V.quantize_mx(T.qw[:], T.sw[:], T.wt[:]), "q_w")
+    g.wait_ge(S.q_w, 1)
+    ship(A, T.le, T.les, E_A, T.qw, T.sw, 2 * EX, S.a_e)
+
+    H = EV // 2
+    V.wait_ge(S.bas, 2)
+    V.wait_ge(S.sm, 1)
+    vec(V.tensor_scalar(T.offo[:], T.base[:], T.selm[:, rank:rank + 1], None, op.add), "offo")
+    vec(V.tensor_scalar(T.sela[:], T.selm[:, A:A + 1], float(SL * (SECOND - A)) / EV, None, op.mult), "sel_a")
+    for q in (V, A_):
+        q.wait_ge(S.offo, 1)
+        q.wait_ge(S.ld_w, 32)
+    vec(V.tensor_copy(T.ho[:, 0:H], T.wt[:].indirect(T.offo[:, 0:16])), "g_o")
+    vec(A_.activation(T.ho[:, H:EV], T.wt[:].indirect(T.offo[:, 16:32]), copy), "g_o")
+    V.wait_ge(S.g_o, 2)
+    vec(V.quantize_mx(T.qo[:], T.so[:], T.ho[:]), "q_o")
+
+    def cols(eng, tile, d, k, ts, sem):
+        o = T.off[:, 12 * d:12 * (d + k)]
+        for t in ts:
+            out, win = tile[:, t:k * OV:4], T.xt[:, t:4 * NX].indirect(o)
+            vec(V.tensor_copy(out, win) if eng is V else A_.activation(out, win, copy), sem)
+
+    for q in (V, A_):
+        q.wait_ge(S.off, 4)
+        q.wait_ge(S.ld_x, 16)
+    cols(V, T.ha, A, 1, (0, 1), "g_a")
+    cols(A_, T.ha, A, 1, (2, 3), "g_a")
+    V.wait_ge(S.g_a, 4)
+    vec(V.quantize_mx(T.qa[:], T.sa[:], T.ha[:]), "q_a")
+    g.wait_ge(S.q_a, 1)
+    ship(A, T.lc, T.lcs, CAP * rank, T.qa, T.sa, CAP, S.a_a)
+    cols(V, T.hbp, bp, 2, (0, 1), "g_bp")
+    cols(A_, T.hbp, bp, 2, (2, 3), "g_bp")
+    V.wait_ge(S.g_bp, 4)
+    vec(V.quantize_mx(T.qbp[:], T.sbp[:], T.hbp[:]), "q_bp")
+    g.wait_ge(S.q_bp, 1)
+    ship_bp(T.lc, T.lcs, T.qbp, T.sbp, CAP, ((jb, CAP * rank, S.a_b), (jp, CAP * rank, S.a_p)))
+    cols(A_, T.hx, rank, 1, (0, 1), "g_x")
+    V.wait_ge(S.a_mb, nf)
+    vec(V.tensor_scalar(T.offb[:], T.base[:], T.msgb[:], None, op.add), "offb")
+    V.wait_ge(S.a_mp, npe)
+    vec(V.tensor_scalar(T.offp[:], T.base[:], T.msgp[:], None, op.add), "offp")
+    A_.wait_ge(S.offb, 1)
+    vec(A_.activation(T.he[:, 0:EV], T.wt[:].indirect(T.offb[:]), copy), "g_e")
+    V.wait_ge(S.offp, 1)
+    vec(V.tensor_copy(T.he[:, EV:2 * EV], T.wt[:].indirect(T.offp[:])), "g_e")
+    V.wait_ge(S.g_e, 2)
+    vec(V.quantize_mx(T.qe[:], T.se[:], T.he[:]), "q_e")
+    g.wait_ge(S.q_e, 1)
+    ship_bp(T.le, T.les, T.qe, T.se, EX, ((0, E_B, S.a_eb), (EX, E_P, S.a_ep)))
+    cols(A_, T.hx, rank, 1, (2,), "g_x")
+    cols(V, T.hx, rank, 1, (3,), "g_x")
+    V.wait_ge(S.g_x, 4)
+    vec(V.quantize_mx(T.lc[:, CAP * rank:CAP * rank + CAP], T.lcs[:, CAP * rank:CAP * rank + CAP], T.hx[:]), "q_x")
+
+    V.wait_ge(S.ld_pl, 64)
+    vec(V.tensor_scalar(T.t1[:], T.rawo[:], float(SL), None, op.mult), "t1d")
+    V.wait_ge(S.sel_a, 1)
+    vec(V.tensor_scalar(T.t2[:], T.rawo[:], float(A), T.sela[0:32, :], op.is_equal, op.mult), "t2d")
+    V.wait_ge(S.t1d, 1)
+    vec(V.tensor_tensor(T.t3[:], T.t1[:], T.rawp[:], op.add), "t3d")
+    V.wait_ge(S.t2d, 1)
+    V.wait_ge(S.t3d, 1)
+    vec(V.tensor_tensor(T.t4[:], T.t3[:], T.t2[:], op.add), "t4d")
+    V.wait_ge(S.t4d, 1)
+    for a in range(4):
+        vec(V.tensor_copy(T.offy[32 * a:32 * a + 32, :], T.t4[:]), "offy")
+
+    own = (T.qo, T.so, 0, rank)
+    a0 = (T.le, T.les, E_A, A)
+    a1 = (T.le, T.les, E_A + EX, SECOND)
+    eb = (T.le, T.les, E_B, B)
+    ep = (T.le, T.les, E_P, P)
+    nmm = [0]
+
+    def prod(e, d, bank, eng, ev):
+        q, s, j, b = e
+        sem = S["mm%d" % nmm[0]]
+        nmm[0] += 1
+        c0, n = CAP * d, 2 * CAP
+        ps = T["ps%d" % bank]
+        TE.matmul_mx(ps[:, 0:n], q[:, j:j + EX], s[:, j:j + EX], T.lc[:, c0:c0 + n], T.lcs[:, c0:c0 + n],
+                     True, True).then_inc(sem, 1)
+        w0 = SL * b + c0
+        eng.wait_ge(sem, 1)
+        if eng is V:
+            V.tensor_copy(T.win[:, w0:w0 + n], ps[:, 0:n]).then_inc(S[ev], 1)
+        else:
+            A_.activation(T.win[:, w0:w0 + n], ps[:, 0:n], copy).then_inc(S[ev], 1)
+
+    TE.wait_ge(S.q_o, 1)
+    TE.wait_ge(S.q_x, 1)
+    TE.wait_ge(S.a_e, 2 * nf)
+    TE.wait_ge(S.a_a, 2 * nf)
+    prod(own, oa, 0, A_, "ev1")
+    prod(a0, oa, 1, V, "ev1")
+    prod(a1, oa, 2, A_, "ev1")
+    TE.wait_ge(S.a_b, 2 * nf)
+    TE.wait_ge(S.a_p, 2 * npe)
+    prod(own, bp, 3, V, "ev2")
+    prod(a0, bp, 4, A_, "ev2")
+    prod(a1, bp, 5, V, "ev2")
+    TE.wait_ge(S.a_ep, 2 * npe)
+    prod(ep, oa, 6, A_, "ev3")
+    prod(ep, bp, 7, V, "ev3")
+    TE.wait_ge(S.ev1, 3)
+    TE.wait_ge(S.a_eb, 2 * nf)
+    prod(eb, oa, 0, A_, "ev4")
+    prod(eb, bp, 1, V, "ev4")
+
+    for q in (V, A_):
+        q.wait_ge(S.offy, 4)
+        q.wait_ge(S.ev1, 3)
+        q.wait_ge(S.ev2, 3)
+        q.wait_ge(S.ev3, 2)
+        q.wait_ge(S.ev4, 2)
+    h = NX // 2
+    V.tensor_copy(T.yt[:, 0:h], T.win[:].indirect(T.offy[:, 0:16])).then_inc(S.g_y1, 1)
+    A_.activation(T.yt[:, h:NX], T.win[:].indirect(T.offy[:, 16:32]), copy).then_inc(S.g_y2, 1)
+    SY.wait_ge(S.g_y1, 1)
+    SY.dma_start(T.y[:, 0:h], T.yt[:, 0:h]).then_inc(S.st_a, 16)
+    A_.wait_ge(S.g_y2, 1)
+    A_.dma_start(T.y[:, h:NX], T.yt[:, h:NX]).then_inc(S.st_b, 16)
+    SY.wait_ge(S.st_a, 16)
+    A_.wait_ge(S.st_b, 16)
+    g.wait_ge(S.sent, n_sent[0])

@@ -6,61 +6,54 @@ NX = 512
 EX = 128
 SL = 4 * CAP
 EV, OV = 4 * EX, 4 * CAP
-
-E_A, E_B, E_P = 0, 2 * EX, 3 * EX
-SECOND = 4
+NPROD = 12
 
 CODE = "float8_e4m3fn_x4"
 SCRATCH = {
     "raws": ("sbuf", [32, 48], "int32"),
     "rawp": ("sbuf", [32, 32], "int32"),
     "rawo": ("sbuf", [32, 32], "int32"),
-    "selr": ("sbuf", [128, 16], "int32"),
-    "self1": ("sbuf", [128, 16], "float32"),
-    "selm": ("sbuf", [128, 16], "float32"),
-    "sela": ("sbuf", [128, 1], "float32"),
+    "selr": ("sbuf", [1, 16], "int32"),
+    "self1": ("sbuf", [1, 4], "float32"),
+    "msga": ("sbuf", [128, 1], "float32"),
+    "msgb": ("sbuf", [128, 1], "float32"),
+    "selm": ("sbuf", [128, 4], "float32"),
+    "selp": ("sbuf", [32, 1], "float32"),
     "ia": ("sbuf", [128, 32], "int32"),
     "ib": ("sbuf", [128, 32], "int32"),
     "ic": ("sbuf", [128, 32], "int32"),
     "base": ("sbuf", [128, 32], "float32"),
     "off": ("sbuf", [128, 48], "uint16"),
-    "offo": ("sbuf", [128, 32], "uint16"),
-    "offp": ("sbuf", [128, 32], "uint16"),
-    "offb": ("sbuf", [128, 32], "uint16"),
     "offy": ("sbuf", [128, 32], "uint16"),
-    "t1": ("sbuf", [32, 32], "float32"),
+    "t1": ("sbuf", [32, 32], "int32"),
     "t2": ("sbuf", [32, 32], "float32"),
     "t3": ("sbuf", [32, 32], "float32"),
-    "t4": ("sbuf", [32, 32], "float32"),
-    "msgp": ("sbuf", [128, 1], "float32"),
-    "msgb": ("sbuf", [128, 1], "float32"),
     "xt": ("sbuf", [128, 4 * NX], "bfloat16"),
     "wt": ("sbuf", [128, 2 * EV], "bfloat16"),
-    "ho": ("sbuf", [128, EV], "bfloat16"),
-    "he": ("sbuf", [128, 2 * EV], "bfloat16"),
-    "ha": ("sbuf", [128, OV], "bfloat16"),
-    "hbp": ("sbuf", [128, 2 * OV], "bfloat16"),
-    "hx": ("sbuf", [128, OV], "bfloat16"),
+    "hc": ("sbuf", [128, 4 * SL], "bfloat16"),
+    "qc": ("sbuf", [128, SL], CODE), "sc": ("sbuf", [128, SL], "uint8"),
     "qw": ("sbuf", [128, 2 * EX], CODE), "sw": ("sbuf", [128, 2 * EX], "uint8"),
-    "qe": ("sbuf", [128, 2 * EX], CODE), "se": ("sbuf", [128, 2 * EX], "uint8"),
-    "qo": ("sbuf", [128, EX], CODE), "so": ("sbuf", [128, EX], "uint8"),
-    "qa": ("sbuf", [128, CAP], CODE), "sa": ("sbuf", [128, CAP], "uint8"),
-    "qbp": ("sbuf", [128, 2 * CAP], CODE), "sbp": ("sbuf", [128, 2 * CAP], "uint8"),
-    "le": ("sbuf", [128, 4 * EX], CODE), "les": ("sbuf", [128, 4 * EX], "uint8"),
-    "lc": ("sbuf", [128, SL], CODE), "lcs": ("sbuf", [128, SL], "uint8"),
+    "lw": ("sbuf", [128, 2 * EX], CODE), "lws": ("sbuf", [128, 2 * EX], "uint8"),
+    "lc": ("sbuf", [128, SL], CODE), "sa": ("sbuf", [128, EX + CAP], "uint8"),
+    "lsa": ("sbuf", [128, EX + 2 * CAP], "uint8"), "lsb": ("sbuf", [128, 2 * CAP], "uint8"),
     "win": ("sbuf", [128, 5 * SL], "float32"),
     "yt": ("sbuf", [128, NX], "float32"),
 }
+for _k in range(4):
+    SCRATCH["eo%d" % _k] = ("sbuf", [128, 32], "uint16")
+    SCRATCH["eh%d" % _k] = ("sbuf", [128, EV], "bfloat16")
+    SCRATCH["eq%d" % _k] = ("sbuf", [128, EX], CODE)
+    SCRATCH["es%d" % _k] = ("sbuf", [128, EX], "uint8")
+    SCRATCH["le%d" % _k] = ("sbuf", [128, EX], CODE)
+    SCRATCH["ls%d" % _k] = ("sbuf", [128, EX], "uint8")
 for _k in range(8):
     SCRATCH["ps%d" % _k] = ("psum", [128, 512], "float32")
 
-SEMAPHORES = ["ld_sel", "ld_send", "ld_w", "ld_x", "ld_pl", "st_a", "st_b",
-              "io", "io2", "bas", "sf", "sm", "off", "offo", "offp", "offb", "offy", "sel_a",
-              "t1d", "t2d", "t3d", "t4d",
-              "q_w", "q_e", "q_o", "q_a", "q_bp", "q_x",
-              "g_o", "g_a", "g_bp", "g_e", "g_x", "g_y1", "g_y2",
-              "sent", "a_mp", "a_mb", "a_e", "a_a", "a_p", "a_b", "a_eb", "a_ep",
-              "ev1", "ev2", "ev3", "ev4"] + ["mm%d" % k for k in range(10)]
+SEMAPHORES = ["ld_sel", "ld_send", "ld_w", "ld_x", "ld_pl", "io", "io2", "bas", "sf", "sm", "a_ma", "a_mb", "off", "offy", "sel_p",
+              "t1d", "t2d", "t3d", "t4d", "q_w", "a_w", "sent"]
+SEMAPHORES += ["%s%d" % (n, k) for n in ("g_c", "q_c", "eo", "g_e", "q_e", "a_c", "a_e", "g_y", "st")
+               for k in range(4)]
+SEMAPHORES += ["%s%d" % (n, k) for n in ("mm", "ev") for k in range(18)] + ["ev_last"]
 
 
 def rank_program(g, core, T, topo):
@@ -77,32 +70,57 @@ def rank_program(g, core, T, topo):
     far = [d for d in others if d != P]
     A = [d for d in far if topo.die(T.cores[d]) == topo.die(core)][0]
     B = [d for d in far if d != A][0]
-    assert abs(rank - A) == 1 and abs(B - P) == 1
-    oa, bp = min(rank, A), min(B, P)
-    jb, jp = CAP * (B - bp), CAP * (P - bp)
+    assert abs(B - P) == 1
+    bp = min(B, P)
     eng_far = topo.engines(core, T.cores[B])
     eng_p = [e for e in topo.engines(core, T.cores[P]) if e not in eng_far]
-    m_far = sum(1 << e for e in eng_far)
-    m_p = sum(1 << e for e in eng_p)
-    nf, npe = len(eng_far), len(eng_p)
+    engines = {A: eng_far, B: eng_far, P: eng_p}
+    half = len(eng_far) // 2
+    n_sent = [0]
 
-    def dst(d):
-        rid, pid, _ = topo.addr(T.cores[d])
-        return rid, pid
+    def write(parts, rsem):
+        if len(parts) == 1:
+            d, es, land, src = parts[0]
+            rid, pid, _ = topo.addr(T.cores[d])
+            g.remote_dma(land, src, S[rsem], S.sent, pid, rid, sum(1 << e for e in es))
+            n_sent[0] += len(es)
+            return
+        transfers = []
+        for d, es, land, src in parts:
+            rid, pid, _ = topo.addr(T.cores[d])
+            transfers.append(RemoteDMATransfer(dst_ids=[DstId(rid=rid, pnc=pid)], remote_sem=S[rsem], src=src, dst=land,
+                                               dma_engine_mask=sum(1 << e for e in es)))
+            n_sent[0] += len(es)
+        g.remote_dma_fused(transfers, local_sem=S.sent)
+
+    def raw(view):
+        return view.bitcast(dt.uint8)
 
     def vec(inst, sem, n=1):
         inst.then_inc(S[sem], n)
 
-    SY.dma_start(T.selr[0:1, 0:16], T.sel[:]).then_inc(S.ld_sel, 16)
+    def move(eng, out, in_, sem):
+        vec(V.tensor_copy(out, in_) if eng is V else A_.activation(out, in_, copy), sem)
+
+    oa, low = min(rank, A), rank < A
+    sa_e, sa_c = (0, EX) if low else (CAP, 0)
+    land_a = 0 if low else CAP
+    lsa_e, lsa_c = (2 * CAP, 0) if low else (0, EX)
+
+    def plane(c0, n):
+        if CAP * oa <= c0 < CAP * oa + 2 * CAP:
+            return T.lsa[:, lsa_c + c0 - CAP * oa:lsa_c + c0 - CAP * oa + n]
+        return T.lsb[:, c0 - CAP * bp:c0 - CAP * bp + n]
+
+    SY.dma_start(T.selr[:], T.sel[:]).then_inc(S.ld_sel, 16)
+    A_.dma_start(T.raws[0:16, :], T.send[:]).then_inc(S.ld_send, 16)
     A_.dma_start(T.raws[16:32, :], T.send[:]).then_inc(S.ld_send, 16)
-    SY.dma_start(T.raws[0:16, :], T.send[:]).then_inc(S.ld_send, 16)
-    A_.dma_start(T.rawp[0:16, :], T.place[:]).then_inc(S.ld_pl, 16)
-    SY.dma_start(T.rawp[16:32, :], T.place[:]).then_inc(S.ld_pl, 16)
-    A_.dma_start(T.rawo[0:16, :], T.of[:]).then_inc(S.ld_pl, 16)
+    SY.dma_start(T.xt[:], T.x[:]).then_inc(S.ld_x, 16)
     for k in range(2):
         SY.dma_start(T.wt[:, EV * k:EV * k + EV], T.w[128 * k:128 * k + 128, :]).then_inc(S.ld_w, 16)
-    A_.dma_start(T.rawo[16:32, :], T.of[:]).then_inc(S.ld_pl, 16)
-    SY.dma_start(T.xt[:], T.x[:]).then_inc(S.ld_x, 16)
+    for a in range(2):
+        A_.dma_start(T.rawp[16 * a:16 * a + 16, :], T.place[:]).then_inc(S.ld_pl, 16)
+        A_.dma_start(T.rawo[16 * a:16 * a + 16, :], T.of[:]).then_inc(S.ld_pl, 16)
 
     g.iota(T.ia[:], [[16, 32]], 0, 1).then_inc(S["io"], 1)
     g.iota(T.ic[:], [[16, 32]], 0, 0).then_inc(S.io2, 1)
@@ -113,162 +131,167 @@ def rank_program(g, core, T, topo):
     vec(V.tensor_tensor(T.base[:], T.ib[:], T.ic[:], op.add), "bas")
 
     V.wait_ge(S.ld_sel, 16)
-    vec(V.tensor_scalar(T.self1[0:1, :], T.selr[0:1, :], 0.0, float(EV), op.max, op.mult), "sf")
+    vec(V.tensor_scalar(T.self1[:], T.selr[:, 0:4], 0.0, float(EV), op.max, op.mult), "sf")
     g.wait_ge(S.sf, 1)
-    g.partition_broadcast(T.selm[:], T.self1[0:1, :], 128).then_inc(S.sm, 1)
+    g.partition_broadcast(T.selm[:], T.self1[:], 128).then_inc(S.sm, 1)
     g.wait_ge(S.sm, 1)
-    for d, msg, rsem, mask in ((B, T.msgb, S.a_mb, m_far), (P, T.msgp, S.a_mp, m_p)):
-        rid, pid = dst(d)
-        g.remote_dma(msg[:], T.selm[:, d:d + 1], rsem, S.sent, pid, rid, mask)
-    n_sent = [nf + npe]
+    write([(A, eng_far, T.msga[:], T.selm[:, A:A + 1])], "a_ma")
+    write([(B, eng_far, T.msgb[:], T.selm[:, B:B + 1])], "a_mb")
 
-    def ship(d, lq, ls, l0, q, s, n, rsem):
-        rid, pid = dst(d)
-        g.remote_dma(lq[:, l0:l0 + n].bitcast(dt.uint8), q[:, 0:n].bitcast(dt.uint8), rsem, S.sent, pid, rid, m_far)
-        g.remote_dma(ls[:, l0:l0 + n], s[:, 0:n], rsem, S.sent, pid, rid, m_far)
-        n_sent[0] += 2 * nf
+    def slots(eng, ds, ts):
+        a, b = min(ds), max(ds) + 1
+        for t in ts:
+            move(eng, T.hc[:, OV * a + t:OV * b:4], T.xt[:, t:4 * NX].indirect(T.off[:, 12 * a:12 * b]), "g_c%d" % a)
 
-    def ship_bp(lq, ls, q, s, n, from_to):
-        for src, land, codes in ((q, lq, True), (s, ls, False)):
-            tr = []
-            for d, m, (j, l, rs) in zip((B, P), (m_far, m_p), from_to):
-                a, b = src[:, j:j + n], land[:, l:l + n]
-                if codes:
-                    a, b = a.bitcast(dt.uint8), b.bitcast(dt.uint8)
-                rid, pid = dst(d)
-                tr.append(RemoteDMATransfer(dst_ids=[DstId(rid=rid, pnc=pid)], dma_engine_mask=m, remote_sem=rs,
-                                            src=a, dst=b))
-            g.remote_dma_fused(tr, local_sem=S.sent)
-        n_sent[0] += 2 * (nf + npe)
+    def pack_slots(ds):
+        a, b = min(ds), max(ds) + 1
+        V.wait_ge(S["g_c%d" % a], 4)
+        q = T.lc if rank in ds else T.qc
+        s = {rank: plane(CAP * rank, CAP), A: T.sa[:, sa_c:sa_c + CAP]}.get(a, T.sc[:, CAP * a:CAP * b])
+        vec(V.quantize_mx(q[:, CAP * a:CAP * b], s, T.hc[:, OV * a:OV * b]), "q_c%d" % a)
+        if rank not in ds:
+            g.wait_ge(S["q_c%d" % a], 1)
+            write([(a, engines[a], raw(T.lc[:, CAP * rank:CAP * rank + CAP]), raw(q[:, CAP * a:CAP * b]))], "a_c%d" % rank)
+            if a != A:
+                write([(a, engines[a], T.lsb[:, CAP * (rank - oa):CAP * (rank - oa) + CAP], s)], "a_c%d" % rank)
+
+    def choice(d):
+        V.wait_ge(S.bas, 2)
+        sem, n, first = {rank: (S.sm, 1, T.selm[:, d:d + 1]), A: (S.a_ma, len(eng_far), T.msga[:]),
+                         B: (S.a_mb, len(eng_far), T.msgb[:])}[d]
+        V.wait_ge(sem, n)
+        vec(V.tensor_scalar(T["eo%d" % d][:], T.base[:], first, None, op.add), "eo%d" % d)
+
+    def expert(eng, d, c0, c1):
+        eng.wait_ge(S.ld_w, 32)
+        eng.wait_ge(S["eo%d" % d], 1)
+        move(eng, T["eh%d" % d][:, 16 * c0:16 * c1], T.wt[:].indirect(T["eo%d" % d][:, c0:c1]), "g_e%d" % d)
+
+    def pack_expert(d, parts):
+        V.wait_ge(S["g_e%d" % d], parts)
+        s = T.sa[:, sa_e:sa_e + EX] if d == A else T["es%d" % d][:]
+        vec(V.quantize_mx(T["eq%d" % d][:], s, T["eh%d" % d][:]), "q_e%d" % d)
+        if d != rank:
+            g.wait_ge(S["q_e%d" % d], 1)
+            write([(d, engines[d], raw(T["le%d" % rank][:]), raw(T["eq%d" % d][:]))], "a_e%d" % rank)
+            if d == A:
+                write([(d, engines[d], T.lsa[:, land_a:land_a + EX + CAP], T.sa[:])], "a_e%d" % rank)
+            else:
+                write([(d, engines[d], T["ls%d" % rank][:], s)], "a_e%d" % rank)
+
+    def pack_both():
+        V.wait_ge(S.ld_w, 32)
+        vec(V.quantize_mx(T.qw[:], T.sw[:], T.wt[:]), "q_w")
+        g.wait_ge(S.q_w, 1)
+        write([(P, eng_p, raw(T.lw[:]), raw(T.qw[:]))], "a_w")
+        write([(P, eng_p, T.lws[:], T.sw[:])], "a_w")
+
+    def y_offsets(step):
+        if step == 0:
+            V.wait_ge(S.sm, 1)
+            vec(V.tensor_scalar(T.selp[:], T.selm[0:32, P:P + 1], 0.2 / EV, 0.4 - 0.2 * P, op.mult, op.add), "sel_p")
+        if step == 1:
+            V.wait_ge(S.ld_pl, 64)
+            V.wait_ge(S.sel_p, 1)
+            vec(V.tensor_scalar(T.t1[:], T.rawo[:], 1.2, T.selp[:], op.mult, op.add), "t1d")
+        if step == 2:
+            V.wait_ge(S.t1d, 1)
+            vec(V.tensor_scalar(T.t2[:], T.t1[:], float(SL), None, op.mult), "t2d")
+        if step == 3:
+            V.wait_ge(S.t2d, 1)
+            vec(V.tensor_tensor(T.t3[:], T.t2[:], T.rawp[:], op.add), "t3d")
+        if step == 4:
+            V.wait_ge(S.t3d, 1)
+            vec(V.tensor_copy(T.offy[0:32, :], T.t3[:]), "t4d")
+            SY.wait_ge(S.t4d, 1)
+            for a in range(1, 4):
+                SY.dma_start(T.offy[32 * a:32 * a + 32, :], T.offy[0:32, :]).then_inc(S.offy, 16)
 
     V.wait_ge(S.ld_send, 32)
     for a in range(4):
         vec(V.tensor_scalar(T.off[32 * a:32 * a + 32, :], T.raws[:], 4.0, 0.0, op.mult, op.max), "off")
-    V.wait_ge(S.ld_w, 32)
-    vec(V.quantize_mx(T.qw[:], T.sw[:], T.wt[:]), "q_w")
-    g.wait_ge(S.q_w, 1)
-    ship(A, T.le, T.les, E_A, T.qw, T.sw, 2 * EX, S.a_e)
-
-    H = EV // 2
-    V.wait_ge(S.bas, 2)
-    V.wait_ge(S.sm, 1)
-    vec(V.tensor_scalar(T.offo[:], T.base[:], T.selm[:, rank:rank + 1], None, op.add), "offo")
-    vec(V.tensor_scalar(T.sela[:], T.selm[:, A:A + 1], float(SL * (SECOND - A)) / EV, None, op.mult), "sel_a")
-    for q in (V, A_):
-        q.wait_ge(S.offo, 1)
-        q.wait_ge(S.ld_w, 32)
-    vec(V.tensor_copy(T.ho[:, 0:H], T.wt[:].indirect(T.offo[:, 0:16])), "g_o")
-    vec(A_.activation(T.ho[:, H:EV], T.wt[:].indirect(T.offo[:, 16:32]), copy), "g_o")
-    V.wait_ge(S.g_o, 2)
-    vec(V.quantize_mx(T.qo[:], T.so[:], T.ho[:]), "q_o")
-
-    def cols(eng, tile, d, k, ts, sem):
-        o = T.off[:, 12 * d:12 * (d + k)]
-        for t in ts:
-            out, win = tile[:, t:k * OV:4], T.xt[:, t:4 * NX].indirect(o)
-            vec(V.tensor_copy(out, win) if eng is V else A_.activation(out, win, copy), sem)
-
+    choice(rank)
+    y_offsets(0)
     for q in (V, A_):
         q.wait_ge(S.off, 4)
         q.wait_ge(S.ld_x, 16)
-    cols(V, T.ha, A, 1, (0, 1), "g_a")
-    cols(A_, T.ha, A, 1, (2, 3), "g_a")
-    V.wait_ge(S.g_a, 4)
-    vec(V.quantize_mx(T.qa[:], T.sa[:], T.ha[:]), "q_a")
-    g.wait_ge(S.q_a, 1)
-    ship(A, T.lc, T.lcs, CAP * rank, T.qa, T.sa, CAP, S.a_a)
-    cols(V, T.hbp, bp, 2, (0, 1), "g_bp")
-    cols(A_, T.hbp, bp, 2, (2, 3), "g_bp")
-    V.wait_ge(S.g_bp, 4)
-    vec(V.quantize_mx(T.qbp[:], T.sbp[:], T.hbp[:]), "q_bp")
-    g.wait_ge(S.q_bp, 1)
-    ship_bp(T.lc, T.lcs, T.qbp, T.sbp, CAP, ((jb, CAP * rank, S.a_b), (jp, CAP * rank, S.a_p)))
-    cols(A_, T.hx, rank, 1, (0, 1), "g_x")
-    V.wait_ge(S.a_mb, nf)
-    vec(V.tensor_scalar(T.offb[:], T.base[:], T.msgb[:], None, op.add), "offb")
-    V.wait_ge(S.a_mp, npe)
-    vec(V.tensor_scalar(T.offp[:], T.base[:], T.msgp[:], None, op.add), "offp")
-    A_.wait_ge(S.offb, 1)
-    vec(A_.activation(T.he[:, 0:EV], T.wt[:].indirect(T.offb[:]), copy), "g_e")
-    V.wait_ge(S.offp, 1)
-    vec(V.tensor_copy(T.he[:, EV:2 * EV], T.wt[:].indirect(T.offp[:])), "g_e")
-    V.wait_ge(S.g_e, 2)
-    vec(V.quantize_mx(T.qe[:], T.se[:], T.he[:]), "q_e")
-    g.wait_ge(S.q_e, 1)
-    ship_bp(T.le, T.les, T.qe, T.se, EX, ((0, E_B, S.a_eb), (EX, E_P, S.a_ep)))
-    cols(A_, T.hx, rank, 1, (2,), "g_x")
-    cols(V, T.hx, rank, 1, (3,), "g_x")
-    V.wait_ge(S.g_x, 4)
-    vec(V.quantize_mx(T.lc[:, CAP * rank:CAP * rank + CAP], T.lcs[:, CAP * rank:CAP * rank + CAP], T.hx[:]), "q_x")
 
-    V.wait_ge(S.ld_pl, 64)
-    vec(V.tensor_scalar(T.t1[:], T.rawo[:], float(SL), None, op.mult), "t1d")
-    V.wait_ge(S.sel_a, 1)
-    vec(V.tensor_scalar(T.t2[:], T.rawo[:], float(A), T.sela[0:32, :], op.is_equal, op.mult), "t2d")
-    V.wait_ge(S.t1d, 1)
-    vec(V.tensor_tensor(T.t3[:], T.t1[:], T.rawp[:], op.add), "t3d")
-    V.wait_ge(S.t2d, 1)
-    V.wait_ge(S.t3d, 1)
-    vec(V.tensor_tensor(T.t4[:], T.t3[:], T.t2[:], op.add), "t4d")
-    V.wait_ge(S.t4d, 1)
-    for a in range(4):
-        vec(V.tensor_copy(T.offy[32 * a:32 * a + 32, :], T.t4[:]), "offy")
+    slots(A_, [A], (2, 3))
+    slots(A_, [B], (2, 3))
+    slots(A_, [P], (1, 2, 3))
+    expert(A_, A, 0, 20)
+    expert(A_, B, 0, 20)
+    expert(A_, rank, 0, 32)
+    slots(A_, [rank], (2, 3))
 
-    own = (T.qo, T.so, 0, rank)
-    a0 = (T.le, T.les, E_A, A)
-    a1 = (T.le, T.les, E_A + EX, SECOND)
-    eb = (T.le, T.les, E_B, B)
-    ep = (T.le, T.les, E_P, P)
+    slots(V, [A], (0, 1))
+    pack_both()
+    pack_slots([A])
+    slots(V, [B], (0, 1))
+    pack_slots([B])
+    slots(V, [P], (0,))
+    choice(A)
+    expert(V, A, 20, 32)
+    choice(B)
+    pack_slots([P])
+    pack_expert(A, 2)
+    expert(V, B, 20, 32)
+    pack_expert(B, 2)
+    y_offsets(1)
+    slots(V, [rank], (0,))
+    y_offsets(2)
+    pack_expert(rank, 1)
+    y_offsets(3)
+    slots(V, [rank], (1,))
+    y_offsets(4)
+    pack_slots([rank])
+
+    def block(h):
+        return h + (h > P)
+
+    own = (T["eq%d" % rank][:], T["es%d" % rank][:], block(rank))
+    p0 = (T.lw[:, 0:EX], T.lws[:, 0:EX], P)
+    p1 = (T.lw[:, EX:2 * EX], T.lws[:, EX:2 * EX], P + 1)
     nmm = [0]
 
-    def prod(e, d, bank, eng, ev):
-        q, s, j, b = e
-        sem = S["mm%d" % nmm[0]]
+    def prod(e, c0, n, eng):
+        q, s, b = e
+        k = nmm[0]
         nmm[0] += 1
-        c0, n = CAP * d, 2 * CAP
-        ps = T["ps%d" % bank]
-        TE.matmul_mx(ps[:, 0:n], q[:, j:j + EX], s[:, j:j + EX], T.lc[:, c0:c0 + n], T.lcs[:, c0:c0 + n],
-                     True, True).then_inc(sem, 1)
+        ps = T["ps%d" % (k % 8)]
+        if k >= 8:
+            TE.wait_ge(S["ev%d" % (k - 8)], 1)
+        TE.matmul_mx(ps[:, 0:n], q, s, T.lc[:, c0:c0 + n], plane(c0, n), True, True).then_inc(S["mm%d" % k], 1)
         w0 = SL * b + c0
-        eng.wait_ge(sem, 1)
-        if eng is V:
-            V.tensor_copy(T.win[:, w0:w0 + n], ps[:, 0:n]).then_inc(S[ev], 1)
-        else:
-            A_.activation(T.win[:, w0:w0 + n], ps[:, 0:n], copy).then_inc(S[ev], 1)
+        eng.wait_ge(S["mm%d" % k], 1)
+        move(eng, T.win[:, w0:w0 + n], ps[:, 0:n], "ev%d" % k if k + 8 < NPROD else "ev_last")
 
-    TE.wait_ge(S.q_o, 1)
-    TE.wait_ge(S.q_x, 1)
-    TE.wait_ge(S.a_e, 2 * nf)
-    TE.wait_ge(S.a_a, 2 * nf)
-    prod(own, oa, 0, A_, "ev1")
-    prod(a0, oa, 1, V, "ev1")
-    prod(a1, oa, 2, A_, "ev1")
-    TE.wait_ge(S.a_b, 2 * nf)
-    TE.wait_ge(S.a_p, 2 * npe)
-    prod(own, bp, 3, V, "ev2")
-    prod(a0, bp, 4, A_, "ev2")
-    prod(a1, bp, 5, V, "ev2")
-    TE.wait_ge(S.a_ep, 2 * npe)
-    prod(ep, oa, 6, A_, "ev3")
-    prod(ep, bp, 7, V, "ev3")
-    TE.wait_ge(S.ev1, 3)
-    TE.wait_ge(S.a_eb, 2 * nf)
-    prod(eb, oa, 0, A_, "ev4")
-    prod(eb, bp, 1, V, "ev4")
+    TE.wait_ge(S.a_w, 2 * len(eng_p))
+    ea = (T["le%d" % A][:], T.lsa[:, lsa_e:lsa_e + EX], block(A))
+    eb = (T["le%d" % B][:], T["ls%d" % B][:], block(B))
+    for d in (B, P):
+        TE.wait_ge(S["a_c%d" % d], 2 * len(engines[d]))
+    prod(p0, CAP * bp, 2 * CAP, A_)
+    prod(p1, CAP * bp, 2 * CAP, V)
+    TE.wait_ge(S["q_e%d" % rank], 1)
+    prod(own, CAP * bp, 2 * CAP, A_)
+    TE.wait_ge(S["a_c%d" % A], len(eng_far))
+    TE.wait_ge(S["a_e%d" % A], 2 * len(eng_far))
+    prod(ea, CAP * bp, 2 * CAP, V)
+    TE.wait_ge(S["q_c%d" % rank], 1)
+    for e, eng in ((p0, A_), (p1, V), (own, A_), (ea, V)):
+        prod(e, CAP * oa, 2 * CAP, eng)
+    TE.wait_ge(S["a_e%d" % B], 2 * len(eng_far))
+    for c0, n, eng in ((0, 256, A_), (384, 256, V), (256, 128, A_), (640, 128, V)):
+        prod(eb, c0, n, eng)
+    assert nmm[0] == NPROD
 
-    for q in (V, A_):
-        q.wait_ge(S.offy, 4)
-        q.wait_ge(S.ev1, 3)
-        q.wait_ge(S.ev2, 3)
-        q.wait_ge(S.ev3, 2)
-        q.wait_ge(S.ev4, 2)
     h = NX // 2
-    V.tensor_copy(T.yt[:, 0:h], T.win[:].indirect(T.offy[:, 0:16])).then_inc(S.g_y1, 1)
-    A_.activation(T.yt[:, h:NX], T.win[:].indirect(T.offy[:, 16:32]), copy).then_inc(S.g_y2, 1)
-    SY.wait_ge(S.g_y1, 1)
-    SY.dma_start(T.y[:, 0:h], T.yt[:, 0:h]).then_inc(S.st_a, 16)
-    A_.wait_ge(S.g_y2, 1)
-    A_.dma_start(T.y[:, h:NX], T.yt[:, h:NX]).then_inc(S.st_b, 16)
-    SY.wait_ge(S.st_a, 16)
-    A_.wait_ge(S.st_b, 16)
+    for k, eng in enumerate((V, A_)):
+        eng.wait_ge(S.offy, 3 * 16)
+        eng.wait_ge(S.ev_last, 8)
+        move(eng, T.yt[:, h * k:h * k + h], T.win[:].indirect(T.offy[:, 16 * k:16 * k + 16]), "g_y0")
+    SY.wait_ge(S.g_y0, 2)
+    SY.dma_start(T.y[:], T.yt[:]).then_inc(S.st0, 16)
+    SY.wait_ge(S.st0, 16)
     g.wait_ge(S.sent, n_sent[0])

from concourse.bass import DstId, RemoteDMATransfer
from concourse.mybir import dt, AluOpType, ActivationFunctionType

CAP = 192
NX = 512
EX = 128
SL = 4 * CAP
EV, OV = 4 * EX, 4 * CAP
NPROD = 12

CODE = "float8_e4m3fn_x4"
SCRATCH = {
    "raws": ("sbuf", [32, 48], "int32"),
    "rawp": ("sbuf", [32, 32], "int32"),
    "rawo": ("sbuf", [32, 32], "int32"),
    "selr": ("sbuf", [1, 16], "int32"),
    "self1": ("sbuf", [1, 4], "float32"),
    "msga": ("sbuf", [128, 1], "float32"),
    "msgb": ("sbuf", [128, 1], "float32"),
    "selm": ("sbuf", [128, 4], "float32"),
    "selp": ("sbuf", [32, 1], "float32"),
    "ia": ("sbuf", [128, 32], "int32"),
    "ib": ("sbuf", [128, 32], "int32"),
    "ic": ("sbuf", [128, 32], "int32"),
    "base": ("sbuf", [128, 32], "float32"),
    "off": ("sbuf", [128, 48], "uint16"),
    "offy": ("sbuf", [128, 32], "uint16"),
    "t1": ("sbuf", [32, 32], "int32"),
    "t2": ("sbuf", [32, 32], "float32"),
    "t3": ("sbuf", [32, 32], "float32"),
    "xt": ("sbuf", [128, 4 * NX], "bfloat16"),
    "wt": ("sbuf", [128, 2 * EV], "bfloat16"),
    "hc": ("sbuf", [128, 4 * SL], "bfloat16"),
    "qc": ("sbuf", [128, SL], CODE), "sc": ("sbuf", [128, SL], "uint8"),
    "qw": ("sbuf", [128, 2 * EX], CODE), "sw": ("sbuf", [128, 2 * EX], "uint8"),
    "lw": ("sbuf", [128, 2 * EX], CODE), "lws": ("sbuf", [128, 2 * EX], "uint8"),
    "lc": ("sbuf", [128, SL], CODE), "sa": ("sbuf", [128, EX + CAP], "uint8"),
    "lsa": ("sbuf", [128, EX + 2 * CAP], "uint8"), "lsb": ("sbuf", [128, 2 * CAP], "uint8"),
    "win": ("sbuf", [128, 5 * SL], "float32"),
    "yt": ("sbuf", [128, NX], "float32"),
}
for _k in range(4):
    SCRATCH["eo%d" % _k] = ("sbuf", [128, 32], "uint16")
    SCRATCH["eh%d" % _k] = ("sbuf", [128, EV], "bfloat16")
    SCRATCH["eq%d" % _k] = ("sbuf", [128, EX], CODE)
    SCRATCH["es%d" % _k] = ("sbuf", [128, EX], "uint8")
    SCRATCH["le%d" % _k] = ("sbuf", [128, EX], CODE)
    SCRATCH["ls%d" % _k] = ("sbuf", [128, EX], "uint8")
for _k in range(8):
    SCRATCH["ps%d" % _k] = ("psum", [128, 512], "float32")

SEMAPHORES = ["ld_sel", "ld_send", "ld_w", "ld_x", "ld_pl", "io", "io2", "bas", "sf", "sm", "a_ma", "a_mb", "off", "offy", "sel_p",
              "t1d", "t2d", "t3d", "t4d", "q_w", "a_w", "sent"]
SEMAPHORES += ["%s%d" % (n, k) for n in ("g_c", "q_c", "eo", "g_e", "q_e", "a_c", "a_e", "g_y", "st")
               for k in range(4)]
SEMAPHORES += ["%s%d" % (n, k) for n in ("mm", "ev") for k in range(18)] + ["ev_last"]


def rank_program(g, core, T, topo):
    rank = T.rank_of(core)
    if rank is None:
        return
    S = T.sem
    V, A_, TE, SY = g.vector, g.scalar, g.tensor, g.sync
    op = AluOpType
    copy = ActivationFunctionType.Copy

    others = [d for d in range(len(T.cores)) if d != rank]
    P = [d for d in others if topo.chip(T.cores[d]) == topo.chip(core)][0]
    far = [d for d in others if d != P]
    A = [d for d in far if topo.die(T.cores[d]) == topo.die(core)][0]
    B = [d for d in far if d != A][0]
    assert abs(B - P) == 1
    bp = min(B, P)
    eng_far = topo.engines(core, T.cores[B])
    eng_p = [e for e in topo.engines(core, T.cores[P]) if e not in eng_far]
    engines = {A: eng_far, B: eng_far, P: eng_p}
    half = len(eng_far) // 2
    n_sent = [0]

    def write(parts, rsem):
        if len(parts) == 1:
            d, es, land, src = parts[0]
            rid, pid, _ = topo.addr(T.cores[d])
            g.remote_dma(land, src, S[rsem], S.sent, pid, rid, sum(1 << e for e in es))
            n_sent[0] += len(es)
            return
        transfers = []
        for d, es, land, src in parts:
            rid, pid, _ = topo.addr(T.cores[d])
            transfers.append(RemoteDMATransfer(dst_ids=[DstId(rid=rid, pnc=pid)], remote_sem=S[rsem], src=src, dst=land,
                                               dma_engine_mask=sum(1 << e for e in es)))
            n_sent[0] += len(es)
        g.remote_dma_fused(transfers, local_sem=S.sent)

    def raw(view):
        return view.bitcast(dt.uint8)

    def vec(inst, sem, n=1):
        inst.then_inc(S[sem], n)

    def move(eng, out, in_, sem):
        vec(V.tensor_copy(out, in_) if eng is V else A_.activation(out, in_, copy), sem)

    oa, low = min(rank, A), rank < A
    sa_e, sa_c = (0, EX) if low else (CAP, 0)
    land_a = 0 if low else CAP
    lsa_e, lsa_c = (2 * CAP, 0) if low else (0, EX)

    def plane(c0, n):
        if CAP * oa <= c0 < CAP * oa + 2 * CAP:
            return T.lsa[:, lsa_c + c0 - CAP * oa:lsa_c + c0 - CAP * oa + n]
        return T.lsb[:, c0 - CAP * bp:c0 - CAP * bp + n]

    SY.dma_start(T.selr[:], T.sel[:]).then_inc(S.ld_sel, 16)
    A_.dma_start(T.raws[0:16, :], T.send[:]).then_inc(S.ld_send, 16)
    A_.dma_start(T.raws[16:32, :], T.send[:]).then_inc(S.ld_send, 16)
    SY.dma_start(T.xt[:], T.x[:]).then_inc(S.ld_x, 16)
    for k in range(2):
        SY.dma_start(T.wt[:, EV * k:EV * k + EV], T.w[128 * k:128 * k + 128, :]).then_inc(S.ld_w, 16)
    for a in range(2):
        A_.dma_start(T.rawp[16 * a:16 * a + 16, :], T.place[:]).then_inc(S.ld_pl, 16)
        A_.dma_start(T.rawo[16 * a:16 * a + 16, :], T.of[:]).then_inc(S.ld_pl, 16)

    g.iota(T.ia[:], [[16, 32]], 0, 1).then_inc(S["io"], 1)
    g.iota(T.ic[:], [[16, 32]], 0, 0).then_inc(S.io2, 1)
    V.wait_ge(S["io"], 1)
    vec(V.tensor_scalar(T.ib[:], T.ia[:], 15, None, op.bitwise_and), "bas")
    V.wait_ge(S["bas"], 1)
    V.wait_ge(S.io2, 1)
    vec(V.tensor_tensor(T.base[:], T.ib[:], T.ic[:], op.add), "bas")

    V.wait_ge(S.ld_sel, 16)
    vec(V.tensor_scalar(T.self1[:], T.selr[:, 0:4], 0.0, float(EV), op.max, op.mult), "sf")
    g.wait_ge(S.sf, 1)
    g.partition_broadcast(T.selm[:], T.self1[:], 128).then_inc(S.sm, 1)
    g.wait_ge(S.sm, 1)
    write([(A, eng_far, T.msga[:], T.selm[:, A:A + 1])], "a_ma")
    write([(B, eng_far, T.msgb[:], T.selm[:, B:B + 1])], "a_mb")

    def slots(eng, ds, ts):
        a, b = min(ds), max(ds) + 1
        for t in ts:
            move(eng, T.hc[:, OV * a + t:OV * b:4], T.xt[:, t:4 * NX].indirect(T.off[:, 12 * a:12 * b]), "g_c%d" % a)

    def pack_slots(ds):
        a, b = min(ds), max(ds) + 1
        V.wait_ge(S["g_c%d" % a], 4)
        q = T.lc if rank in ds else T.qc
        s = {rank: plane(CAP * rank, CAP), A: T.sa[:, sa_c:sa_c + CAP]}.get(a, T.sc[:, CAP * a:CAP * b])
        vec(V.quantize_mx(q[:, CAP * a:CAP * b], s, T.hc[:, OV * a:OV * b]), "q_c%d" % a)
        if rank not in ds:
            g.wait_ge(S["q_c%d" % a], 1)
            write([(a, engines[a], raw(T.lc[:, CAP * rank:CAP * rank + CAP]), raw(q[:, CAP * a:CAP * b]))], "a_c%d" % rank)
            if a != A:
                write([(a, engines[a], T.lsb[:, CAP * (rank - oa):CAP * (rank - oa) + CAP], s)], "a_c%d" % rank)

    def choice(d):
        V.wait_ge(S.bas, 2)
        sem, n, first = {rank: (S.sm, 1, T.selm[:, d:d + 1]), A: (S.a_ma, len(eng_far), T.msga[:]),
                         B: (S.a_mb, len(eng_far), T.msgb[:])}[d]
        V.wait_ge(sem, n)
        vec(V.tensor_scalar(T["eo%d" % d][:], T.base[:], first, None, op.add), "eo%d" % d)

    def expert(eng, d, c0, c1):
        eng.wait_ge(S.ld_w, 32)
        eng.wait_ge(S["eo%d" % d], 1)
        move(eng, T["eh%d" % d][:, 16 * c0:16 * c1], T.wt[:].indirect(T["eo%d" % d][:, c0:c1]), "g_e%d" % d)

    def pack_expert(d, parts):
        V.wait_ge(S["g_e%d" % d], parts)
        s = T.sa[:, sa_e:sa_e + EX] if d == A else T["es%d" % d][:]
        vec(V.quantize_mx(T["eq%d" % d][:], s, T["eh%d" % d][:]), "q_e%d" % d)
        if d != rank:
            g.wait_ge(S["q_e%d" % d], 1)
            write([(d, engines[d], raw(T["le%d" % rank][:]), raw(T["eq%d" % d][:]))], "a_e%d" % rank)
            if d == A:
                write([(d, engines[d], T.lsa[:, land_a:land_a + EX + CAP], T.sa[:])], "a_e%d" % rank)
            else:
                write([(d, engines[d], T["ls%d" % rank][:], s)], "a_e%d" % rank)

    def pack_both():
        V.wait_ge(S.ld_w, 32)
        vec(V.quantize_mx(T.qw[:], T.sw[:], T.wt[:]), "q_w")
        g.wait_ge(S.q_w, 1)
        write([(P, eng_p, raw(T.lw[:]), raw(T.qw[:]))], "a_w")
        write([(P, eng_p, T.lws[:], T.sw[:])], "a_w")

    def y_offsets(step):
        if step == 0:
            V.wait_ge(S.sm, 1)
            vec(V.tensor_scalar(T.selp[:], T.selm[0:32, P:P + 1], 0.2 / EV, 0.4 - 0.2 * P, op.mult, op.add), "sel_p")
        if step == 1:
            V.wait_ge(S.ld_pl, 64)
            V.wait_ge(S.sel_p, 1)
            vec(V.tensor_scalar(T.t1[:], T.rawo[:], 1.2, T.selp[:], op.mult, op.add), "t1d")
        if step == 2:
            V.wait_ge(S.t1d, 1)
            vec(V.tensor_scalar(T.t2[:], T.t1[:], float(SL), None, op.mult), "t2d")
        if step == 3:
            V.wait_ge(S.t2d, 1)
            vec(V.tensor_tensor(T.t3[:], T.t2[:], T.rawp[:], op.add), "t3d")
        if step == 4:
            V.wait_ge(S.t3d, 1)
            vec(V.tensor_copy(T.offy[0:32, :], T.t3[:]), "t4d")
            SY.wait_ge(S.t4d, 1)
            for a in range(1, 4):
                SY.dma_start(T.offy[32 * a:32 * a + 32, :], T.offy[0:32, :]).then_inc(S.offy, 16)

    V.wait_ge(S.ld_send, 32)
    for a in range(4):
        vec(V.tensor_scalar(T.off[32 * a:32 * a + 32, :], T.raws[:], 4.0, 0.0, op.mult, op.max), "off")
    choice(rank)
    y_offsets(0)
    for q in (V, A_):
        q.wait_ge(S.off, 4)
        q.wait_ge(S.ld_x, 16)

    slots(A_, [A], (2, 3))
    slots(A_, [B], (2, 3))
    slots(A_, [P], (1, 2, 3))
    expert(A_, A, 0, 20)
    expert(A_, B, 0, 20)
    expert(A_, rank, 0, 32)
    slots(A_, [rank], (2, 3))

    slots(V, [A], (0, 1))
    pack_both()
    pack_slots([A])
    slots(V, [B], (0, 1))
    pack_slots([B])
    slots(V, [P], (0,))
    choice(A)
    expert(V, A, 20, 32)
    choice(B)
    pack_slots([P])
    pack_expert(A, 2)
    expert(V, B, 20, 32)
    pack_expert(B, 2)
    y_offsets(1)
    slots(V, [rank], (0,))
    y_offsets(2)
    pack_expert(rank, 1)
    y_offsets(3)
    slots(V, [rank], (1,))
    y_offsets(4)
    pack_slots([rank])

    def block(h):
        return h + (h > P)

    own = (T["eq%d" % rank][:], T["es%d" % rank][:], block(rank))
    p0 = (T.lw[:, 0:EX], T.lws[:, 0:EX], P)
    p1 = (T.lw[:, EX:2 * EX], T.lws[:, EX:2 * EX], P + 1)
    nmm = [0]

    def prod(e, c0, n, eng):
        q, s, b = e
        k = nmm[0]
        nmm[0] += 1
        ps = T["ps%d" % (k % 8)]
        if k >= 8:
            TE.wait_ge(S["ev%d" % (k - 8)], 1)
        TE.matmul_mx(ps[:, 0:n], q, s, T.lc[:, c0:c0 + n], plane(c0, n), True, True).then_inc(S["mm%d" % k], 1)
        w0 = SL * b + c0
        eng.wait_ge(S["mm%d" % k], 1)
        move(eng, T.win[:, w0:w0 + n], ps[:, 0:n], "ev%d" % k if k + 8 < NPROD else "ev_last")

    TE.wait_ge(S.a_w, 2 * len(eng_p))
    ea = (T["le%d" % A][:], T.lsa[:, lsa_e:lsa_e + EX], block(A))
    eb = (T["le%d" % B][:], T["ls%d" % B][:], block(B))
    for d in (B, P):
        TE.wait_ge(S["a_c%d" % d], 2 * len(engines[d]))
    prod(p0, CAP * bp, 2 * CAP, A_)
    prod(p1, CAP * bp, 2 * CAP, V)
    TE.wait_ge(S["q_e%d" % rank], 1)
    prod(own, CAP * bp, 2 * CAP, A_)
    TE.wait_ge(S["a_c%d" % A], len(eng_far))
    TE.wait_ge(S["a_e%d" % A], 2 * len(eng_far))
    prod(ea, CAP * bp, 2 * CAP, V)
    TE.wait_ge(S["q_c%d" % rank], 1)
    for e, eng in ((p0, A_), (p1, V), (own, A_), (ea, V)):
        prod(e, CAP * oa, 2 * CAP, eng)
    TE.wait_ge(S["a_e%d" % B], 2 * len(eng_far))
    for c0, n, eng in ((0, 256, A_), (384, 256, V), (256, 128, A_), (640, 128, V)):
        prod(eb, c0, n, eng)
    assert nmm[0] == NPROD

    h = NX // 2
    for k, eng in enumerate((V, A_)):
        eng.wait_ge(S.offy, 3 * 16)
        eng.wait_ge(S.ev_last, 8)
        move(eng, T.yt[:, h * k:h * k + h], T.win[:].indirect(T.offy[:, 16 * k:16 * k + 16]), "g_y0")
    SY.wait_ge(S.g_y0, 2)
    SY.dma_start(T.y[:], T.yt[:]).then_inc(S.st0, 16)
    SY.wait_ge(S.st0, 16)
    g.wait_ge(S.sent, n_sent[0])
